import numpy as np
import ml_dtypes


def mxq(x, axis, fmt="e4m3"):
    dtype, down = {"e4m3": (ml_dtypes.float8_e4m3fn, 7), "e5m2": (ml_dtypes.float8_e5m2, 14)}[fmt]
    v = np.moveaxis(np.asarray(x, np.float32).astype(ml_dtypes.bfloat16).astype(np.float64), axis, -1)
    blocks = v.reshape(v.shape[:-1] + (-1, 32))
    amax = np.abs(blocks).max(-1, keepdims=True)
    byte = np.maximum(np.where(amax > 0, np.frexp(amax)[1] - 1 + 127, 0) - down, 1)
    scale = np.exp2(byte - 127.0)
    codes = (blocks / scale).astype(np.float32).astype(dtype).astype(np.float64)
    return np.moveaxis((codes * scale).reshape(v.shape), -1, axis)


WIDE = False


def mx_kscale(k):
    if not WIDE:
        return np.ones(k)
    levels = np.array([10, -10, 5, -5, 0])
    if k % 512:
        return np.exp2(np.random.permutation(np.resize(levels, k // 32))).repeat(32)
    a = np.empty((k // 512, 16))
    for p in range(k // 512):
        a[p, :8] = np.random.permutation(np.resize(levels, 8))
        for g in range(8):
            far = levels[np.abs(levels - a[p, g]) >= 10]
            a[p, g + 8] = far[np.random.randint(len(far))]
    return np.exp2(a.ravel()).repeat(32)


def f64(x):
    return np.asarray(x).astype(np.float64)


def striped(idx):
    return np.tile(idx.reshape(-1, 16).T, (8, 1)).astype(np.uint16)


def unstriped(offs):
    return offs[:16].T.reshape(-1).astype(np.int64)


def pack_weight(w):
    k, n = w.shape
    w = f64(np.asarray(w, np.float32).astype(ml_dtypes.bfloat16)).reshape(k // 32, 32, n)
    amax = np.abs(w).max(1)
    byte = np.clip(np.where(amax > 0, np.frexp(amax)[1] - 1 + 127 - 7, 1), 1, 254)
    scaled = (w * np.exp2(127.0 - byte)[:, None, :]).reshape(k, n).astype(np.float32)
    words = np.ascontiguousarray(scaled.reshape(k // 512, 128, 4, n).transpose(0, 1, 3, 2)).astype(ml_dtypes.float8_e4m3fn).view(np.uint8)
    return words, np.ascontiguousarray(byte.astype(np.uint8).reshape(k // 512, 16, n))


def unpack_weight(words, scales):
    g, p, n, _ = words.shape
    vals = np.ascontiguousarray(words).view(ml_dtypes.float8_e4m3fn).astype(np.float64) * np.repeat(np.exp2(scales.astype(np.float64) - 127.0), 8, axis=1)[..., None]
    return vals.transpose(0, 1, 3, 2).reshape(g * 512, n)


E2M1 = np.array([0.0, 0.5, 1.0, 1.5, 2.0, 3.0, 4.0, 6.0, -0.0, -0.5, -1.0, -1.5, -2.0, -3.0, -4.0, -6.0])


def pack_fp4(w):
    k, n = w.shape
    w = f64(np.asarray(w, np.float32).astype(ml_dtypes.bfloat16)).reshape(k // 32, 32, n)
    amax = np.abs(w).max(1)
    mant, ex = np.frexp(amax / 6.0)
    byte = np.clip(np.where(amax > 0, np.where(mant > 0.5, ex, ex - 1) + 127, 1), 1, 254)
    scaled = (w * np.exp2(127.0 - byte)[:, None, :]).reshape(k, n).astype(np.float32)
    c = np.ascontiguousarray(scaled.reshape(k // 512, 128, 4, n).transpose(0, 1, 3, 2)).astype(ml_dtypes.float4_e2m1fn).view(np.uint8) & 0xF
    words = (c[..., 0::2] | (c[..., 1::2] << 4)).reshape(k // 512, 128, 2 * n)
    return np.ascontiguousarray(words), np.ascontiguousarray(byte.astype(np.uint8).reshape(k // 512, 16, n))


def unpack_fp4(words, scales):
    g, _, n = scales.shape
    words = np.ascontiguousarray(words).reshape(g, 128, n, 2)
    nib = np.empty((g, 128, n, 4), np.uint8)
    nib[..., 0::2] = words & 0xF
    nib[..., 1::2] = words >> 4
    vals = E2M1[nib] * np.repeat(np.exp2(scales.astype(np.float64) - 127.0), 8, axis=1)[..., None]
    return vals.transpose(0, 1, 3, 2).reshape(g * 512, n)


def planes(y):
    n, m = y.shape
    v = y.astype(np.float32).astype(ml_dtypes.bfloat16).astype(np.float64).reshape(n // 32, 32, m)
    top = np.abs(v).max(1)
    byte = np.clip(np.where(top > 0, np.frexp(top)[1] - 1 + 127 - 7, 1), 1, 254)
    codes = (v * np.exp2(127.0 - byte)[:, None, :]).reshape(n, m).astype(np.float32).astype(ml_dtypes.float8_e4m3fn).view(np.uint8)
    words = codes.reshape(n // 512, 128, 4, m).transpose(0, 1, 3, 2)
    return np.ascontiguousarray(words), np.ascontiguousarray(byte.astype(np.uint8).reshape(n // 512, 16, m))


def sigmoid(v):
    return 1.0 / (1.0 + np.exp(-np.maximum(v, -700.0)))


K, T, S, D, N, H, V, U = 1024, 2048, 512, 2, 512, 512, 256, 512


def setup_inputs():
    n = np.random.standard_normal
    s = mx_kscale(K)[:, None]
    u = mx_kscale(H)
    packed_xT = pack_weight(n((K, T)) * s)
    packed_w1 = pack_fp4(n((K, N)) / np.sqrt(K) / s)
    packed_w2 = pack_fp4(n((K, N)) / np.sqrt(K) / s)
    packed_w3 = pack_fp4(n((H, N)) / np.sqrt(H) / u[:, None])
    return {
        "x_words": packed_xT[0],
        "x_scales": packed_xT[1],
        "w1_words": packed_w1[0],
        "w1_scales": packed_w1[1],
        "w2_words": packed_w2[0],
        "w2_scales": packed_w2[1],
        "own": (n((H, U))).astype(np.float32),
        "unit": (np.random.uniform(0.6, 1.4, (H, 1)) * u[:, None]).astype(np.float32),
        "w3_words": packed_w3[0],
        "w3_scales": packed_w3[1],
        "offs": striped(np.random.permutation(T)[:S]),
        "root": striped(np.random.permutation(np.concatenate([np.arange(V), np.random.randint(0, V, U - V)]))),
        "leaf": striped(np.random.permutation(np.concatenate([np.arange(V), np.random.randint(0, V, U - V)]))),
        "sib": striped(np.random.permutation(U)),
    }


def reference(x_words, x_scales, w1_words, w1_scales, w2_words, w2_scales, own, unit, w3_words, w3_scales, offs, root, leaf, sib):
    xq = unpack_weight(x_words, x_scales)[:, unstriped(offs)]
    y = unpack_fp4(w1_words, w1_scales).T @ xq
    ys = unpack_fp4(w2_words, w2_scales).T @ xq
    yg2 = y * sigmoid(ys)
    pref = yg2.reshape(len(yg2), -1, D).sum(axis=2)
    rt_ = pref[:, unstriped(root)]
    lf = pref[:, unstriped(leaf)]
    path = rt_ + lf * np.tanh(rt_)
    hid = f64(unit) * (path * f64(own) + lf[:, unstriped(sib)])
    out_0 = unpack_fp4(w3_words, w3_scales).T @ mxq(hid, 0, "e4m3")
    return (out_0,) + planes(out_0)

@@ -1,0 +1,278 @@
+from contextlib import ExitStack
+
+import concourse.mybir as mybir
+
+K, T, S, H, N, V, U = 1024, 2048, 512, 512, 512, 256, 512
+FLOPS = 2 * (2 * K * N * S + H * N * U)
+
+F32 = mybir.dt.float32
+BF16 = mybir.dt.bfloat16
+I32 = mybir.dt.int32
+U32 = mybir.dt.uint32
+U16 = mybir.dt.uint16
+U8 = mybir.dt.uint8
+FP8X4 = mybir.dt.float8_e4m3fn_x4
+FP4X4 = mybir.dt.float4_e2m1fn_x4
+ACT = mybir.ActivationFunctionType
+ALU = mybir.AluOpType
+
+P = 128
+PACK = 4
+PASSES = K // (P * PACK)
+CH = 128
+NCH = U // CH
+LC = CH // 16
+
+
+def tile_picked_yprefsh_own_po_kernel(
+    tc, x_words, x_scales, w1_words, w1_scales, w2_words, w2_scales, own, unit, w3_words, w3_scales,
+    offs, root, leaf, sib, out_0, out_1, out_2,
+):
+    nc = tc.nc
+    with ExitStack() as ctx:
+        keep = ctx.enter_context(tc.tile_pool(name="keep", bufs=1))
+        ring = ctx.enter_context(tc.tile_pool(name="ring", bufs=2))
+        psum = ctx.enter_context(tc.psum_pool(name="psum", bufs=1))
+
+        def load_list(src, name):
+            tile = keep.tile([P, src.shape[1]], U16, name=name)
+            nc.sync.dma_start(tile[:], src)
+            return tile
+
+        def scale_tile(engine, width, name):
+            tile = keep.tile([P, width], U8, name=name, align_bytes=64)
+            engine.memset(tile[:].bitcast(I32), 0)
+            return tile
+
+        def load_scale_rows(queue, src, tile):
+            passes, width = src.shape[0], src.shape[2]
+            for q in range(4):
+                queue.dma_start(
+                    tile[32 * q : 32 * q + 4, : passes * width].bitcast(I32).rearrange("r (o c) -> r o c", o=passes),
+                    src[:, 4 * q : 4 * q + 4, :].bitcast(I32).rearrange("o r c -> r o c"),
+                )
+
+        def load_fp4_words(src, name, tag):
+            passes, width = src.shape[0], src.shape[2]
+            tile = keep.tile([P, passes * width], U8, name=name, tag=tag, align_bytes=64)
+            nc.sync.dma_start(
+                tile[:].bitcast(I32).rearrange("p (o c) -> p o c", o=passes),
+                src.bitcast(I32).rearrange("o p c -> p o c"),
+            )
+            return tile
+
+        def deal(raw, passes, dtype, size, name):
+            tile = keep.tile([P, passes, PACK, P * size], U8, name=name, align_bytes=64)
+            nc.vector.tensor_copy(
+                tile[:].bitcast(dtype),
+                raw[:, : passes * PACK * P * size].bitcast(dtype).rearrange("p (o m t) -> p o t m", o=passes, t=PACK),
+            )
+            return tile
+
+        offs_sb = load_list(offs, "offs_sb")
+        leaf_sb = load_list(leaf, "leaf_sb")
+        root_sb = load_list(root, "root_sb")
+        sib_sb = load_list(sib, "sib_sb")
+        w2w_raw = load_fp4_words(w2_words, "w2w_raw", "wide1")
+        w1w_raw = load_fp4_words(w1_words, "w1w_raw", "raw_words")
+
+        def load_x_words(o):
+            tile = keep.tile([P, T], I32, name=f"xw_raw{o}", tag=f"wide{o}", align_bytes=64)
+            nc.sync.dma_start(tile[:], x_words[o].rearrange("p c r -> p (c r)").bitcast(I32))
+            return tile
+
+        xw_raw0 = load_x_words(0)
+        xs_raw = scale_tile(nc.vector, PASSES * T, "xs_raw")
+        w2s_raw = scale_tile(nc.gpsimd, PASSES * N, "w2s_raw")
+        w1s_raw = scale_tile(nc.vector, PASSES * N, "w1s_raw")
+        load_scale_rows(nc.scalar, x_scales, xs_raw)
+        load_scale_rows(nc.gpsimd, w2_scales, w2s_raw)
+        load_scale_rows(nc.scalar, w1_scales, w1s_raw)
+        unit_sb = keep.tile([P, PACK], F32, name="unit_sb")
+        nc.gpsimd.dma_start(unit_sb[:], unit.rearrange("(p t) o -> p (t o)", t=PACK))
+
+        xs = [keep.tile([P, S], U8, name=f"xs{o}", align_bytes=64) for o in range(PASSES)]
+        xw = [keep.tile([P, S], U32, name=f"xw{o}", align_bytes=64) for o in range(PASSES)]
+
+        def pick_scales(o):
+            nc.vector.tensor_copy(xs[o][:], xs_raw[:, o * T : (o + 1) * T].indirect(offs_sb[:]))
+
+        def pick_words(o, raw):
+            nc.vector.tensor_copy(xw[o][:], raw[:].bitcast(U32).indirect(offs_sb[:]))
+
+        w2w = deal(w2w_raw, PASSES, U16, 2, "w2w")
+        xw_raw1 = load_x_words(1)
+        w1w = deal(w1w_raw, PASSES, U16, 2, "w1w")
+        w3w_raw = load_fp4_words(w3_words, "w3w_raw", "raw_words")
+        pick_scales(0)
+        pick_words(0, xw_raw0)
+        own_sb = keep.tile([P, PACK, U], F32, name="own_sb", tag="wide0", align_bytes=64)
+        nc.sync.dma_start(own_sb[:], own.rearrange("(p t) j -> p t j", t=PACK))
+        w2s = deal(w2s_raw, PASSES, U8, 1, "w2s")
+        load_scale_rows(nc.sync, w3_scales, w2s_raw)
+        w3s_raw = w2s_raw
+        w1s = deal(w1s_raw, PASSES, U8, 1, "w1s")
+        pick_scales(1)
+        pick_words(1, xw_raw1)
+
+        ys = [psum.tile([P, S], F32, name=f"ys{t}", tag=f"bank{t}") for t in range(PACK)]
+        y = [psum.tile([P, S], F32, name=f"y{t}", tag=f"bank{PACK + t}") for t in range(PACK)]
+        for t in range(PACK):
+            for o in range(PASSES):
+                for bank, words, scales in ((ys[t], w2w, w2s), (y[t], w1w, w1s)):
+                    nc.tensor.matmul_mx(
+                        out=bank[:],
+                        lhsT=words[:, o, t, :].bitcast(FP4X4),
+                        lhsT_scale=scales[:, o, t, :],
+                        rhs=xw[o][:].bitcast(FP8X4),
+                        rhs_scale=xs[o][:],
+                        start=(o == 0),
+                        stop=(o == PASSES - 1),
+                    )
+
+        root_window = [keep.tile([P, V + S], F32, name=f"root_window{t}") for t in range(PACK)]
+        leaf_window = [keep.tile([P, V + S], F32, name=f"leaf_window{t}") for t in range(PACK)]
+        lf = [keep.tile([P, U], F32, name=f"lf{t}") for t in range(PACK)]
+        rt = [keep.tile([P, U], F32, name=f"rt{t}") for t in range(PACK)]
+        th = [keep.tile([P, U], F32, name=f"th{t}") for t in range(PACK)]
+
+        def by_member(ap):
+            return ap.rearrange("p (d v) -> p d v", d=2)
+
+        for t in range(PACK):
+            nc.scalar.activation(by_member(leaf_window[t][:, V:]), ys[t][:].rearrange("p (v d) -> p d v", d=2), ACT.Sigmoid)
+
+        for step in range(PACK + 2):
+            if step < PACK:
+                t = step
+                nc.vector.tensor_tensor(
+                    by_member(root_window[t][:, V:]),
+                    y[t][:].rearrange("p (v d) -> p d v", d=2),
+                    by_member(leaf_window[t][:, V:]),
+                    ALU.mult,
+                )
+            if 1 <= step <= PACK:
+                t = step - 1
+                nc.vector.tensor_tensor(root_window[t][:, :V], root_window[t][:, V : 2 * V], root_window[t][:, 2 * V :], ALU.add)
+            if step >= 2:
+                t = step - 2
+                nc.vector.tensor_scalar(leaf_window[t][:, :V], root_window[t][:, :V], unit_sb[:, t : t + 1], None, ALU.mult)
+        for t in range(PACK):
+            nc.scalar.activation(rt[t][:], root_window[t][:].indirect(root_sb[:]), ACT.Copy)
+            nc.scalar.activation(lf[t][:], leaf_window[t][:].indirect(leaf_sb[:]), ACT.Copy)
+            nc.scalar.activation(th[t][:], rt[t][:], ACT.Tanh)
+
+        w3w = deal(w3w_raw, 1, U16, 2, "w3w")
+        w3s = deal(w3s_raw, 1, U8, 1, "w3s")
+
+        HALF = U // 2
+        halves = [slice(0, HALF), slice(HALF, U)]
+        sib_halves = [sib_sb[:, : HALF // 16], sib_sb[:, HALF // 16 :]]
+        hid = [keep.tile([P, PACK, HALF], F32, name=f"hid{k}") for k in range(2)]
+        last = PACK - 1
+        sibling = keep.tile([P, U], F32, name="sibling")
+        for k in range(2):
+            nc.scalar.activation(sibling[:, halves[k]], lf[last][:].indirect(sib_halves[k]), ACT.Copy)
+
+        weighted, path, suffixed = {}, {}, {}
+
+        def weigh(t, cols):
+            nc.vector.tensor_tensor(weighted[t][:, cols], lf[t][:, cols], th[t][:, cols], ALU.mult)
+
+        def join(t, cols):
+            nc.vector.scalar_tensor_tensor(
+                path[t][:, cols], rt[t][:, cols], unit_sb[:, t : t + 1], weighted[t][:, cols], ALU.mult, ALU.add
+            )
+
+        def suffix(t, cols):
+            nc.vector.tensor_tensor(suffixed[t][:, cols], path[t][:, cols], own_sb[:, t, cols], ALU.mult)
+
+        def add_sibling(t, k):
+            if t == last:
+                nc.vector.tensor_tensor(hid[k][:, t, :], sibling[:, halves[k]], suffixed[t][:, halves[k]], ALU.add)
+            else:
+                nc.vector.tensor_tensor(hid[k][:, t, :], lf[t][:].indirect(sib_halves[k]), suffixed[t][:, halves[k]], ALU.add)
+
+        out_codes = keep.tile([P, U], U32, name="out_codes", align_bytes=64)
+        out_scales = keep.tile([P, U], U8, name="out_scales", align_bytes=64)
+        hid_codes = keep.tile([P, U], U32, name="hid_codes", align_bytes=64)
+        hid_scales = keep.tile([P, U], U8, name="hid_scales", align_bytes=64)
+        out_rows = out_0.rearrange("(p t) j -> p t j", t=PACK)
+        out_words = out_1[0].rearrange("p c r -> p (c r)").bitcast(I32)
+        hid_bf, res, res_bf = {}, {}, {}
+
+        def interleave(copy, dst, src):
+            copy(dst.rearrange("p (c i t) -> p c t i", i=4, t=PACK), src.rearrange("p t (c i) -> p c t i", i=4))
+
+        def round_hidden(h, copy):
+            k, start = divmod(h * CH, HALF)
+            hid_bf[h] = keep.tile([P, CH * PACK], BF16, name=f"hid_bf{h}", align_bytes=64)
+            interleave(copy, hid_bf[h][:], hid[k][:, :, start : start + CH])
+
+        def last_product(h):
+            cols = slice(h * CH, (h + 1) * CH)
+            nc.vector.quantize_mx(out=hid_codes[:, cols].bitcast(FP8X4), scales=hid_scales[:, cols], in_=hid_bf[h][:])
+            acc = psum.tile([P, PACK, CH], F32, name=f"acc{h}", tag=f"bank{h}")
+            for t in range(PACK):
+                nc.tensor.matmul_mx(
+                    out=acc[:, t, :],
+                    lhsT=w3w[:, 0, t, :].bitcast(FP4X4),
+                    lhsT_scale=w3s[:, 0, t, :],
+                    rhs=hid_codes[:, cols].bitcast(FP8X4),
+                    rhs_scale=hid_scales[:, cols],
+                    start=True,
+                    stop=True,
+                )
+            res[h] = keep.tile([P, PACK, CH], F32, name=f"res{h}")
+            nc.scalar.copy(res[h][:], acc[:])
+            nc.sync.dma_start(out_rows[:, :, cols], res[h][:])
+
+        def round_result(h):
+            res_bf[h] = keep.tile([P, CH * PACK], BF16, name=f"res_bf{h}", align_bytes=64)
+            interleave(nc.vector.tensor_copy, res_bf[h][:], res[h][:])
+
+        def planes(h):
+            cols = slice(h * CH, (h + 1) * CH)
+            nc.vector.quantize_mx(out=out_codes[:, cols].bitcast(FP8X4), scales=out_scales[:, cols], in_=res_bf[h][:])
+            nc.sync.dma_start(out_words[:, cols], out_codes[:, cols].bitcast(I32))
+
+        whole = slice(0, U)
+        for t in range(PACK):
+            weighted[t] = ring.tile([P, U], F32, name="weighted")
+            path[t] = ring.tile([P, U], F32, name="path")
+            suffixed[t] = ring.tile([P, U], F32, name="suffixed")
+            cols = halves[0] if t == last else whole
+            weigh(t, cols)
+            if t > 0:
+                add_sibling(t - 1, 0)
+            join(t, cols)
+            if t > 0:
+                add_sibling(t - 1, 1)
+            suffix(t, cols)
+        weigh(last, halves[1])
+        add_sibling(last, 0)
+        round_hidden(0, nc.scalar.copy)
+        round_hidden(1, nc.scalar.copy)
+        join(last, halves[1])
+        last_product(0)
+        suffix(last, halves[1])
+        last_product(1)
+        add_sibling(last, 1)
+        round_hidden(2, nc.scalar.copy)
+        round_result(0)
+        round_hidden(3, nc.vector.tensor_copy)
+        planes(0)
+        last_product(2)
+        round_result(1)
+        last_product(3)
+        planes(1)
+        round_result(2)
+        round_result(3)
+        planes(2)
+        planes(3)
+
+        for q in range(4):
+            queue = nc.scalar if q % 2 else nc.sync
+            queue.dma_start(
+                out_2[0, 4 * q : 4 * q + 4, :].bitcast(I32), out_scales[32 * q : 32 * q + 4, :].bitcast(I32)
+            )

@@ -31,7 +31,6 @@ def tile_picked_yprefsh_own_po_kernel(
     nc = tc.nc
     with ExitStack() as ctx:
         keep = ctx.enter_context(tc.tile_pool(name="keep", bufs=1))
-        ring = ctx.enter_context(tc.tile_pool(name="ring", bufs=2))
         psum = ctx.enter_context(tc.psum_pool(name="psum", bufs=1))
 
         def load_list(src, name):
@@ -39,14 +38,14 @@ def tile_picked_yprefsh_own_po_kernel(
             nc.sync.dma_start(tile[:], src)
             return tile
 
-        def scale_tile(engine, width, name):
-            tile = keep.tile([P, width], U8, name=name, align_bytes=64)
+        def scale_tile(engine, width, name, tag):
+            tile = keep.tile([P, width], U8, name=name, tag=tag, align_bytes=64)
             engine.memset(tile[:].bitcast(I32), 0)
             return tile
 
-        def load_scale_rows(queue, src, tile):
+        def load_scale_rows(queue, src, tile, quadrants):
             passes, width = src.shape[0], src.shape[2]
-            for q in range(4):
+            for q in quadrants:
                 queue.dma_start(
                     tile[32 * q : 32 * q + 4, : passes * width].bitcast(I32).rearrange("r (o c) -> r o c", o=passes),
                     src[:, 4 * q : 4 * q + 4, :].bitcast(I32).rearrange("o r c -> r o c"),
@@ -61,74 +60,93 @@ def tile_picked_yprefsh_own_po_kernel(
             )
             return tile
 
-        def deal(raw, passes, dtype, size, name):
-            tile = keep.tile([P, passes, PACK, P * size], U8, name=name, align_bytes=64)
+        def deal(raw, passes, dtype, size, name, tag):
+            tile = keep.tile([P, passes, PACK, P * size], U8, name=name, tag=tag, align_bytes=64)
             nc.vector.tensor_copy(
                 tile[:].bitcast(dtype),
                 raw[:, : passes * PACK * P * size].bitcast(dtype).rearrange("p (o m t) -> p o t m", o=passes, t=PACK),
             )
             return tile
 
-        offs_sb = load_list(offs, "offs_sb")
-        leaf_sb = load_list(leaf, "leaf_sb")
-        root_sb = load_list(root, "root_sb")
-        sib_sb = load_list(sib, "sib_sb")
-        w2w_raw = load_fp4_words(w2_words, "w2w_raw", "wide1")
-        w1w_raw = load_fp4_words(w1_words, "w1w_raw", "raw_words")
-
         def load_x_words(o):
-            tile = keep.tile([P, T], I32, name=f"xw_raw{o}", tag=f"wide{o}", align_bytes=64)
+            tile = keep.tile([P, T], I32, name=f"xw_raw{o}", tag=f"xw_raw{o}", align_bytes=64)
             nc.sync.dma_start(tile[:], x_words[o].rearrange("p c r -> p (c r)").bitcast(I32))
             return tile
 
+        xs_raw = scale_tile(nc.vector, PASSES * T, "xs_raw", "xs_raw")
+        w2s_raw = scale_tile(nc.vector, PASSES * N, "w2s_raw", "w2s_raw")
+        w1s_raw = scale_tile(nc.vector, PASSES * N, "w1s_raw", "w1s_raw")
+        w3s_raw = scale_tile(nc.gpsimd, N, "w3s_raw", "w3s_raw")
+        offs_sb = load_list(offs, "offs_sb")
+        w2w_raw = load_fp4_words(w2_words, "w2w_raw", "w2w_raw")
+        w1w_raw = load_fp4_words(w1_words, "w1w_raw", "w1w_raw")
+        load_scale_rows(nc.sync, x_scales, xs_raw, (0, 1))
+        load_scale_rows(nc.scalar, x_scales, xs_raw, (2, 3))
         xw_raw0 = load_x_words(0)
-        xs_raw = scale_tile(nc.vector, PASSES * T, "xs_raw")
-        w2s_raw = scale_tile(nc.gpsimd, PASSES * N, "w2s_raw")
-        w1s_raw = scale_tile(nc.vector, PASSES * N, "w1s_raw")
-        load_scale_rows(nc.scalar, x_scales, xs_raw)
-        load_scale_rows(nc.gpsimd, w2_scales, w2s_raw)
-        load_scale_rows(nc.scalar, w1_scales, w1s_raw)
+        load_scale_rows(nc.scalar, w2_scales, w2s_raw, range(4))
+        load_scale_rows(nc.scalar, w1_scales, w1s_raw, range(4))
+        xw_raw1 = load_x_words(1)
+        w3w_raw = load_fp4_words(w3_words, "w3w_raw", "w3w_raw")
+        load_scale_rows(nc.gpsimd, w3_scales, w3s_raw, range(4))
+        root_sb = load_list(root, "root_sb")
+        leaf_sb = load_list(leaf, "leaf_sb")
         unit_sb = keep.tile([P, PACK], F32, name="unit_sb")
-        nc.gpsimd.dma_start(unit_sb[:], unit.rearrange("(p t) o -> p (t o)", t=PACK))
-
-        xs = [keep.tile([P, S], U8, name=f"xs{o}", align_bytes=64) for o in range(PASSES)]
-        xw = [keep.tile([P, S], U32, name=f"xw{o}", align_bytes=64) for o in range(PASSES)]
+        nc.sync.dma_start(unit_sb[:], unit.rearrange("(p t) o -> p (t o)", t=PACK))
+        own_sb = keep.tile([P, PACK, U], F32, name="own_sb")
+        nc.sync.dma_start(own_sb[:], own.rearrange("(p t) j -> p t j", t=PACK))
+        sib_sb = load_list(sib, "sib_sb")
 
         def pick_scales(o):
-            nc.vector.tensor_copy(xs[o][:], xs_raw[:, o * T : (o + 1) * T].indirect(offs_sb[:]))
+            tile = keep.tile([P, S], U8, name=f"xs{o}", align_bytes=64)
+            nc.vector.tensor_copy(tile[:], xs_raw[:, o * T : (o + 1) * T].indirect(offs_sb[:]))
+            return tile
 
-        def pick_words(o, raw):
-            nc.vector.tensor_copy(xw[o][:], raw[:].bitcast(U32).indirect(offs_sb[:]))
+        def pick_words(raw, name, tag):
+            tile = keep.tile([P, S], U32, name=name, tag=tag, align_bytes=64)
+            nc.vector.tensor_copy(tile[:], raw[:].bitcast(U32).indirect(offs_sb[:]))
+            return tile
 
-        w2w = deal(w2w_raw, PASSES, U16, 2, "w2w")
-        xw_raw1 = load_x_words(1)
-        w1w = deal(w1w_raw, PASSES, U16, 2, "w1w")
-        w3w_raw = load_fp4_words(w3_words, "w3w_raw", "raw_words")
-        pick_scales(0)
-        pick_words(0, xw_raw0)
-        own_sb = keep.tile([P, PACK, U], F32, name="own_sb", tag="wide0", align_bytes=64)
-        nc.sync.dma_start(own_sb[:], own.rearrange("(p t) j -> p t j", t=PACK))
-        w2s = deal(w2s_raw, PASSES, U8, 1, "w2s")
-        load_scale_rows(nc.sync, w3_scales, w2s_raw)
-        w3s_raw = w2s_raw
-        w1s = deal(w1s_raw, PASSES, U8, 1, "w1s")
-        pick_scales(1)
-        pick_words(1, xw_raw1)
+        w2w = deal(w2w_raw, PASSES, U16, 2, "w2w", "dealt_words")
+        w1w = deal(w1w_raw, PASSES, U16, 2, "w1w", "w1w")
+        xs = [pick_scales(o) for o in range(PASSES)]
+        xw = [pick_words(xw_raw0, "xw0", "xw0")]
+        def deal_scales(raw, first, out):
+            nc.vector.tensor_copy(out, raw[:].rearrange("p (o m t) -> p o t m", o=PASSES, t=PACK)[:, :, first : first + 2, :])
+            return out
+
+        w2s_early = keep.tile([P, PASSES, 2, P], U8, name="w2s_early", align_bytes=64)
+        w1s_early = keep.tile([P, PASSES, 2, P], U8, name="w1s_early", align_bytes=64)
+        w2s = [deal_scales(w2s_raw, 0, w2s_early[:])]
+        w1s = [deal_scales(w1s_raw, 0, w1s_early[:])]
+        xw.append(pick_words(xw_raw1, "xw1", "xw1"))
+        late = keep.tile([P, 3, PASSES, 2, P], U8, name="late", tag="xw_raw1", align_bytes=64)
+        w2s.append(deal_scales(w2s_raw, 2, late[:, 0]))
+        w1s.append(deal_scales(w1s_raw, 2, late[:, 1]))
+        w3s = late[:, 2].rearrange("p a b m -> p (a b) m")
+        nc.vector.tensor_copy(w3s, w3s_raw[:].rearrange("p (m t) -> p t m", t=PACK))
+        w3w = deal(w3w_raw, 1, U16, 2, "w3w", "w3w")
 
         ys = [psum.tile([P, S], F32, name=f"ys{t}", tag=f"bank{t}") for t in range(PACK)]
         y = [psum.tile([P, S], F32, name=f"y{t}", tag=f"bank{PACK + t}") for t in range(PACK)]
-        for t in range(PACK):
+        def product(bank, words, scales, t):
             for o in range(PASSES):
-                for bank, words, scales in ((ys[t], w2w, w2s), (y[t], w1w, w1s)):
-                    nc.tensor.matmul_mx(
-                        out=bank[:],
-                        lhsT=words[:, o, t, :].bitcast(FP4X4),
-                        lhsT_scale=scales[:, o, t, :],
-                        rhs=xw[o][:].bitcast(FP8X4),
-                        rhs_scale=xs[o][:],
-                        start=(o == 0),
-                        stop=(o == PASSES - 1),
-                    )
+                nc.tensor.matmul_mx(
+                    out=bank[:],
+                    lhsT=words[:, o, t, :].bitcast(FP4X4),
+                    lhsT_scale=scales[t // 2][:, o, t % 2, :],
+                    rhs=xw[o][:].bitcast(FP8X4),
+                    rhs_scale=xs[o][:],
+                    start=(o == 0),
+                    stop=(o == PASSES - 1),
+                )
+
+        for t in (0, 1):
+            product(ys[t], w2w, w2s, t)
+            product(y[t], w1w, w1s, t)
+        for t in (2, 3):
+            product(ys[t], w2w, w2s, t)
+        for t in (2, 3):
+            product(y[t], w1w, w1s, t)
 
         root_window = [keep.tile([P, V + S], F32, name=f"root_window{t}") for t in range(PACK)]
         leaf_window = [keep.tile([P, V + S], F32, name=f"leaf_window{t}") for t in range(PACK)]
@@ -142,56 +160,67 @@ def tile_picked_yprefsh_own_po_kernel(
         for t in range(PACK):
             nc.scalar.activation(by_member(leaf_window[t][:, V:]), ys[t][:].rearrange("p (v d) -> p d v", d=2), ACT.Sigmoid)
 
-        for step in range(PACK + 2):
-            if step < PACK:
-                t = step
-                nc.vector.tensor_tensor(
-                    by_member(root_window[t][:, V:]),
-                    y[t][:].rearrange("p (v d) -> p d v", d=2),
-                    by_member(leaf_window[t][:, V:]),
-                    ALU.mult,
-                )
-            if 1 <= step <= PACK:
-                t = step - 1
-                nc.vector.tensor_tensor(root_window[t][:, :V], root_window[t][:, V : 2 * V], root_window[t][:, 2 * V :], ALU.add)
-            if step >= 2:
-                t = step - 2
-                nc.vector.tensor_scalar(leaf_window[t][:, :V], root_window[t][:, :V], unit_sb[:, t : t + 1], None, ALU.mult)
-        for t in range(PACK):
-            nc.scalar.activation(rt[t][:], root_window[t][:].indirect(root_sb[:]), ACT.Copy)
-            nc.scalar.activation(lf[t][:], leaf_window[t][:].indirect(leaf_sb[:]), ACT.Copy)
-            nc.scalar.activation(th[t][:], rt[t][:], ACT.Tanh)
-
-        w3w = deal(w3w_raw, 1, U16, 2, "w3w")
-        w3s = deal(w3s_raw, 1, U8, 1, "w3s")
-
         HALF = U // 2
+        whole = slice(0, U)
         halves = [slice(0, HALF), slice(HALF, U)]
         sib_halves = [sib_sb[:, : HALF // 16], sib_sb[:, HALF // 16 :]]
+        FUSED = 2
         hid = [keep.tile([P, PACK, HALF], F32, name=f"hid{k}") for k in range(2)]
-        last = PACK - 1
-        sibling = keep.tile([P, U], F32, name="sibling")
-        for k in range(2):
-            nc.scalar.activation(sibling[:, halves[k]], lf[last][:].indirect(sib_halves[k]), ACT.Copy)
+        weighted = [keep.tile([P, U], F32, name=f"weighted{t}") for t in range(PACK)]
+        path = [keep.tile([P, U], F32, name=f"path{t}") for t in range(PACK)]
+        suffixed = [keep.tile([P, U], F32, name=f"suffixed{t}") for t in range(PACK)]
+        sibling = {t: keep.tile([P, U], F32, name=f"sibling{t}") for t in range(FUSED, PACK)}
 
-        weighted, path, suffixed = {}, {}, {}
+        def gate(t):
+            nc.vector.tensor_tensor(
+                by_member(root_window[t][:, V:]),
+                y[t][:].rearrange("p (v d) -> p d v", d=2),
+                by_member(leaf_window[t][:, V:]),
+                ALU.mult,
+            )
+
+        def pair_sum(t):
+            nc.vector.tensor_tensor(root_window[t][:, :V], root_window[t][:, V : 2 * V], root_window[t][:, 2 * V :], ALU.add)
+
+        def scale_nodes(t):
+            nc.vector.tensor_scalar(leaf_window[t][:, :V], root_window[t][:, :V], unit_sb[:, t : t + 1], None, ALU.mult)
+
+        def fetch(out, window, offsets):
+            nc.scalar.activation(out, window[:].indirect(offsets), ACT.Copy)
+
+        def look_up(t):
+            fetch(rt[t][:], root_window[t], root_sb[:])
+            if t > 0:
+                fetch(lf[t][:], leaf_window[t] if t < FUSED else root_window[t], leaf_sb[:])
+            nc.scalar.activation(th[t][:], rt[t][:], ACT.Tanh)
 
         def weigh(t, cols):
             nc.vector.tensor_tensor(weighted[t][:, cols], lf[t][:, cols], th[t][:, cols], ALU.mult)
 
         def join(t, cols):
-            nc.vector.scalar_tensor_tensor(
-                path[t][:, cols], rt[t][:, cols], unit_sb[:, t : t + 1], weighted[t][:, cols], ALU.mult, ALU.add
-            )
+            if t < FUSED:
+                nc.vector.scalar_tensor_tensor(
+                    path[t][:, cols], rt[t][:, cols], unit_sb[:, t : t + 1], weighted[t][:, cols], ALU.mult, ALU.add
+                )
+            else:
+                nc.vector.tensor_tensor(path[t][:, cols], rt[t][:, cols], weighted[t][:, cols], ALU.add)
 
         def suffix(t, cols):
-            nc.vector.tensor_tensor(suffixed[t][:, cols], path[t][:, cols], own_sb[:, t, cols], ALU.mult)
+            if t < FUSED:
+                nc.vector.tensor_tensor(suffixed[t][:, cols], path[t][:, cols], own_sb[:, t, cols], ALU.mult)
+            else:
+                nc.vector.scalar_tensor_tensor(
+                    suffixed[t][:, cols], path[t][:, cols], unit_sb[:, t : t + 1], own_sb[:, t, cols], ALU.mult, ALU.mult
+                )
 
         def add_sibling(t, k):
-            if t == last:
-                nc.vector.tensor_tensor(hid[k][:, t, :], sibling[:, halves[k]], suffixed[t][:, halves[k]], ALU.add)
+            cols = halves[k]
+            if t < FUSED:
+                nc.vector.tensor_tensor(hid[k][:, t, :], lf[t][:].indirect(sib_halves[k]), suffixed[t][:, cols], ALU.add)
             else:
-                nc.vector.tensor_tensor(hid[k][:, t, :], lf[t][:].indirect(sib_halves[k]), suffixed[t][:, halves[k]], ALU.add)
+                nc.vector.scalar_tensor_tensor(
+                    hid[k][:, t, :], sibling[t][:, cols], unit_sb[:, t : t + 1], suffixed[t][:, cols], ALU.mult, ALU.add
+                )
 
         out_codes = keep.tile([P, U], U32, name="out_codes", align_bytes=64)
         out_scales = keep.tile([P, U], U8, name="out_scales", align_bytes=64)
@@ -217,7 +246,7 @@ def tile_picked_yprefsh_own_po_kernel(
                 nc.tensor.matmul_mx(
                     out=acc[:, t, :],
                     lhsT=w3w[:, 0, t, :].bitcast(FP4X4),
-                    lhsT_scale=w3s[:, 0, t, :],
+                    lhsT_scale=w3s[:, t, :],
                     rhs=hid_codes[:, cols].bitcast(FP8X4),
                     rhs_scale=hid_scales[:, cols],
                     start=True,
@@ -234,39 +263,59 @@ def tile_picked_yprefsh_own_po_kernel(
         def planes(h):
             cols = slice(h * CH, (h + 1) * CH)
             nc.vector.quantize_mx(out=out_codes[:, cols].bitcast(FP8X4), scales=out_scales[:, cols], in_=res_bf[h][:])
-            nc.sync.dma_start(out_words[:, cols], out_codes[:, cols].bitcast(I32))
+            if h % 2:
+                nc.sync.dma_start(out_words[:, halves[h // 2]], out_codes[:, halves[h // 2]].bitcast(I32))
 
-        whole = slice(0, U)
-        for t in range(PACK):
-            weighted[t] = ring.tile([P, U], F32, name="weighted")
-            path[t] = ring.tile([P, U], F32, name="path")
-            suffixed[t] = ring.tile([P, U], F32, name="suffixed")
-            cols = halves[0] if t == last else whole
-            weigh(t, cols)
-            if t > 0:
-                add_sibling(t - 1, 0)
-            join(t, cols)
-            if t > 0:
-                add_sibling(t - 1, 1)
-            suffix(t, cols)
-        weigh(last, halves[1])
-        add_sibling(last, 0)
+        gate(0)
+        gate(1)
+        pair_sum(0)
+        pair_sum(1)
+        scale_nodes(0)
+        scale_nodes(1)
+        nc.vector.tensor_copy(lf[0][:], leaf_window[0][:].indirect(leaf_sb[:]))
+        gate(2)
+        look_up(0)
+        look_up(1)
+        weigh(0, whole)
+        gate(3)
+        join(0, whole)
+        pair_sum(2)
+        pair_sum(3)
+        suffix(0, whole)
+        look_up(2)
+        look_up(3)
+        for k in range(2):
+            for t in range(FUSED, PACK):
+                fetch(sibling[t][:, halves[k]], lf[t], sib_halves[k])
+        for t in (1, 2):
+            weigh(t, whole)
+            add_sibling(t - 1, 0)
+            join(t, whole)
+            add_sibling(t - 1, 1)
+            suffix(t, whole)
+        weigh(3, halves[0])
+        weigh(3, halves[1])
+        join(3, halves[0])
+        add_sibling(2, 0)
+        suffix(3, halves[0])
+        join(3, halves[1])
+        add_sibling(3, 0)
         round_hidden(0, nc.scalar.copy)
         round_hidden(1, nc.scalar.copy)
-        join(last, halves[1])
+        suffix(3, halves[1])
+        add_sibling(2, 1)
+        add_sibling(3, 1)
         last_product(0)
-        suffix(last, halves[1])
+        round_hidden(2, nc.vector.tensor_copy)
+        round_hidden(3, nc.scalar.copy)
         last_product(1)
-        add_sibling(last, 1)
-        round_hidden(2, nc.scalar.copy)
         round_result(0)
-        round_hidden(3, nc.vector.tensor_copy)
-        planes(0)
         last_product(2)
-        round_result(1)
         last_product(3)
-        planes(1)
+        planes(0)
+        round_result(1)
         round_result(2)
+        planes(1)
         round_result(3)
         planes(2)
         planes(3)

@@ -76,7 +76,7 @@ def tile_picked_yprefsh_own_po_kernel(
         xs_raw = scale_tile(nc.vector, PASSES * T, "xs_raw", "xs_raw")
         w2s_raw = scale_tile(nc.vector, PASSES * N, "w2s_raw", "w2s_raw")
         w1s_raw = scale_tile(nc.vector, PASSES * N, "w1s_raw", "w1s_raw")
-        w3s_raw = scale_tile(nc.gpsimd, N, "w3s_raw", "w3s_raw")
+        w3s_raw = scale_tile(nc.vector, N, "w3s_raw", "w3s_raw")
         offs_sb = load_list(offs, "offs_sb")
         w2w_raw = load_fp4_words(w2_words, "w2w_raw", "w2w_raw")
         w1w_raw = load_fp4_words(w1_words, "w1w_raw", "w1w_raw")
@@ -85,9 +85,9 @@ def tile_picked_yprefsh_own_po_kernel(
         xw_raw0 = load_x_words(0)
         load_scale_rows(nc.scalar, w2_scales, w2s_raw, range(4))
         load_scale_rows(nc.scalar, w1_scales, w1s_raw, range(4))
+        load_scale_rows(nc.scalar, w3_scales, w3s_raw, range(4))
         xw_raw1 = load_x_words(1)
         w3w_raw = load_fp4_words(w3_words, "w3w_raw", "w3w_raw")
-        load_scale_rows(nc.gpsimd, w3_scales, w3s_raw, range(4))
         root_sb = load_list(root, "root_sb")
         leaf_sb = load_list(leaf, "leaf_sb")
         unit_sb = keep.tile([P, PACK], F32, name="unit_sb")
@@ -119,11 +119,9 @@ def tile_picked_yprefsh_own_po_kernel(
         w2s = [deal_scales(w2s_raw, 0, w2s_early[:])]
         w1s = [deal_scales(w1s_raw, 0, w1s_early[:])]
         xw.append(pick_words(xw_raw1, "xw1", "xw1"))
-        late = keep.tile([P, 3, PASSES, 2, P], U8, name="late", tag="xw_raw1", align_bytes=64)
+        late = keep.tile([P, 2, PASSES, 2, P], U8, name="late", tag="xw_raw1", align_bytes=64)
         w2s.append(deal_scales(w2s_raw, 2, late[:, 0]))
         w1s.append(deal_scales(w1s_raw, 2, late[:, 1]))
-        w3s = late[:, 2].rearrange("p a b m -> p (a b) m")
-        nc.vector.tensor_copy(w3s, w3s_raw[:].rearrange("p (m t) -> p t m", t=PACK))
         w3w = deal(w3w_raw, 1, U16, 2, "w3w", "w3w")
 
         ys = [psum.tile([P, S], F32, name=f"ys{t}", tag=f"bank{t}") for t in range(PACK)]
@@ -231,7 +229,7 @@ def tile_picked_yprefsh_own_po_kernel(
         hid_bf, res, res_bf = {}, {}, {}
 
         def interleave(copy, dst, src):
-            copy(dst.rearrange("p (c i t) -> p c t i", i=4, t=PACK), src.rearrange("p t (c i) -> p c t i", i=4))
+            copy(dst.rearrange("p (c i t) -> p c t i", i=2, t=PACK), src.rearrange("p t (c i) -> p c t i", i=2))
 
         def round_hidden(h, copy):
             k, start = divmod(h * CH, HALF)
@@ -246,7 +244,7 @@ def tile_picked_yprefsh_own_po_kernel(
                 nc.tensor.matmul_mx(
                     out=acc[:, t, :],
                     lhsT=w3w[:, 0, t, :].bitcast(FP4X4),
-                    lhsT_scale=w3s[:, t, :],
+                    lhsT_scale=w3s[:, 0, t, :],
                     rhs=hid_codes[:, cols].bitcast(FP8X4),
                     rhs_scale=hid_scales[:, cols],
                     start=True,
@@ -272,6 +270,7 @@ def tile_picked_yprefsh_own_po_kernel(
         pair_sum(1)
         scale_nodes(0)
         scale_nodes(1)
+        w3s = deal(w3s_raw, 1, U8, 1, "w3s", "w3s")
         nc.vector.tensor_copy(lf[0][:], leaf_window[0][:].indirect(leaf_sb[:]))
         gate(2)
         look_up(0)

from contextlib import ExitStack

import concourse.mybir as mybir

K, T, S, H, N, V, U = 1024, 2048, 512, 512, 512, 256, 512
FLOPS = 2 * (2 * K * N * S + H * N * U)

F32 = mybir.dt.float32
BF16 = mybir.dt.bfloat16
I32 = mybir.dt.int32
U32 = mybir.dt.uint32
U16 = mybir.dt.uint16
U8 = mybir.dt.uint8
FP8X4 = mybir.dt.float8_e4m3fn_x4
FP4X4 = mybir.dt.float4_e2m1fn_x4
ACT = mybir.ActivationFunctionType
ALU = mybir.AluOpType

P = 128
PACK = 4
PASSES = K // (P * PACK)
CH = 128
NCH = U // CH
LC = CH // 16


def tile_picked_yprefsh_own_po_kernel(
    tc, x_words, x_scales, w1_words, w1_scales, w2_words, w2_scales, own, unit, w3_words, w3_scales,
    offs, root, leaf, sib, out_0, out_1, out_2,
):
    nc = tc.nc
    with ExitStack() as ctx:
        keep = ctx.enter_context(tc.tile_pool(name="keep", bufs=1))
        psum = ctx.enter_context(tc.psum_pool(name="psum", bufs=1))

        def load_list(src, name):
            tile = keep.tile([P, src.shape[1]], U16, name=name)
            nc.sync.dma_start(tile[:], src)
            return tile

        def scale_tile(engine, width, name, tag):
            tile = keep.tile([P, width], U8, name=name, tag=tag, align_bytes=64)
            engine.memset(tile[:].bitcast(I32), 0)
            return tile

        def load_scale_rows(queue, src, tile, quadrants):
            passes, width = src.shape[0], src.shape[2]
            for q in quadrants:
                queue.dma_start(
                    tile[32 * q : 32 * q + 4, : passes * width].bitcast(I32).rearrange("r (o c) -> r o c", o=passes),
                    src[:, 4 * q : 4 * q + 4, :].bitcast(I32).rearrange("o r c -> r o c"),
                )

        def load_fp4_words(src, name, tag):
            passes, width = src.shape[0], src.shape[2]
            tile = keep.tile([P, passes * width], U8, name=name, tag=tag, align_bytes=64)
            nc.sync.dma_start(
                tile[:].bitcast(I32).rearrange("p (o c) -> p o c", o=passes),
                src.bitcast(I32).rearrange("o p c -> p o c"),
            )
            return tile

        def deal(raw, passes, dtype, size, name, tag):
            tile = keep.tile([P, passes, PACK, P * size], U8, name=name, tag=tag, align_bytes=64)
            nc.vector.tensor_copy(
                tile[:].bitcast(dtype),
                raw[:, : passes * PACK * P * size].bitcast(dtype).rearrange("p (o m t) -> p o t m", o=passes, t=PACK),
            )
            return tile

        def load_x_words(o):
            tile = keep.tile([P, T], I32, name=f"xw_raw{o}", tag=f"xw_raw{o}", align_bytes=64)
            nc.sync.dma_start(tile[:], x_words[o].rearrange("p c r -> p (c r)").bitcast(I32))
            return tile

        xs_raw = scale_tile(nc.vector, PASSES * T, "xs_raw", "xs_raw")
        w2s_raw = scale_tile(nc.vector, PASSES * N, "w2s_raw", "w2s_raw")
        w1s_raw = scale_tile(nc.vector, PASSES * N, "w1s_raw", "w1s_raw")
        w3s_raw = scale_tile(nc.vector, N, "w3s_raw", "w3s_raw")
        offs_sb = load_list(offs, "offs_sb")
        w2w_raw = load_fp4_words(w2_words, "w2w_raw", "w2w_raw")
        w1w_raw = load_fp4_words(w1_words, "w1w_raw", "w1w_raw")
        load_scale_rows(nc.sync, x_scales, xs_raw, (0, 1))
        load_scale_rows(nc.scalar, x_scales, xs_raw, (2, 3))
        xw_raw0 = load_x_words(0)
        load_scale_rows(nc.scalar, w2_scales, w2s_raw, range(4))
        load_scale_rows(nc.scalar, w1_scales, w1s_raw, range(4))
        load_scale_rows(nc.scalar, w3_scales, w3s_raw, range(4))
        xw_raw1 = load_x_words(1)
        w3w_raw = load_fp4_words(w3_words, "w3w_raw", "w3w_raw")
        root_sb = load_list(root, "root_sb")
        leaf_sb = load_list(leaf, "leaf_sb")
        unit_sb = keep.tile([P, PACK], F32, name="unit_sb")
        nc.sync.dma_start(unit_sb[:], unit.rearrange("(p t) o -> p (t o)", t=PACK))
        own_sb = keep.tile([P, PACK, U], F32, name="own_sb")
        nc.sync.dma_start(own_sb[:], own.rearrange("(p t) j -> p t j", t=PACK))
        sib_sb = load_list(sib, "sib_sb")

        def pick_scales(o):
            tile = keep.tile([P, S], U8, name=f"xs{o}", align_bytes=64)
            nc.vector.tensor_copy(tile[:], xs_raw[:, o * T : (o + 1) * T].indirect(offs_sb[:]))
            return tile

        def pick_words(raw, name, tag):
            tile = keep.tile([P, S], U32, name=name, tag=tag, align_bytes=64)
            nc.vector.tensor_copy(tile[:], raw[:].bitcast(U32).indirect(offs_sb[:]))
            return tile

        w2w = deal(w2w_raw, PASSES, U16, 2, "w2w", "dealt_words")
        w1w = deal(w1w_raw, PASSES, U16, 2, "w1w", "w1w")
        xs = [pick_scales(o) for o in range(PASSES)]
        xw = [pick_words(xw_raw0, "xw0", "xw0")]
        def deal_scales(raw, first, out):
            nc.vector.tensor_copy(out, raw[:].rearrange("p (o m t) -> p o t m", o=PASSES, t=PACK)[:, :, first : first + 2, :])
            return out

        w2s_early = keep.tile([P, PASSES, 2, P], U8, name="w2s_early", align_bytes=64)
        w1s_early = keep.tile([P, PASSES, 2, P], U8, name="w1s_early", align_bytes=64)
        w2s = [deal_scales(w2s_raw, 0, w2s_early[:])]
        w1s = [deal_scales(w1s_raw, 0, w1s_early[:])]
        xw.append(pick_words(xw_raw1, "xw1", "xw1"))
        late = keep.tile([P, 2, PASSES, 2, P], U8, name="late", tag="xw_raw1", align_bytes=64)
        w2s.append(deal_scales(w2s_raw, 2, late[:, 0]))
        w1s.append(deal_scales(w1s_raw, 2, late[:, 1]))
        w3w = deal(w3w_raw, 1, U16, 2, "w3w", "w3w")

        ys = [psum.tile([P, S], F32, name=f"ys{t}", tag=f"bank{t}") for t in range(PACK)]
        y = [psum.tile([P, S], F32, name=f"y{t}", tag=f"bank{PACK + t}") for t in range(PACK)]
        def product(bank, words, scales, t):
            for o in range(PASSES):
                nc.tensor.matmul_mx(
                    out=bank[:],
                    lhsT=words[:, o, t, :].bitcast(FP4X4),
                    lhsT_scale=scales[t // 2][:, o, t % 2, :],
                    rhs=xw[o][:].bitcast(FP8X4),
                    rhs_scale=xs[o][:],
                    start=(o == 0),
                    stop=(o == PASSES - 1),
                )

        for t in (0, 1):
            product(ys[t], w2w, w2s, t)
            product(y[t], w1w, w1s, t)
        for t in (2, 3):
            product(ys[t], w2w, w2s, t)
        for t in (2, 3):
            product(y[t], w1w, w1s, t)

        root_window = [keep.tile([P, V + S], F32, name=f"root_window{t}") for t in range(PACK)]
        leaf_window = [keep.tile([P, V + S], F32, name=f"leaf_window{t}") for t in range(PACK)]
        lf = [keep.tile([P, U], F32, name=f"lf{t}") for t in range(PACK)]
        rt = [keep.tile([P, U], F32, name=f"rt{t}") for t in range(PACK)]
        th = [keep.tile([P, U], F32, name=f"th{t}") for t in range(PACK)]

        def by_member(ap):
            return ap.rearrange("p (d v) -> p d v", d=2)

        for t in range(PACK):
            nc.scalar.activation(by_member(leaf_window[t][:, V:]), ys[t][:].rearrange("p (v d) -> p d v", d=2), ACT.Sigmoid)

        HALF = U // 2
        whole = slice(0, U)
        halves = [slice(0, HALF), slice(HALF, U)]
        sib_halves = [sib_sb[:, : HALF // 16], sib_sb[:, HALF // 16 :]]
        FUSED = 2
        hid = [keep.tile([P, PACK, HALF], F32, name=f"hid{k}") for k in range(2)]
        weighted = [keep.tile([P, U], F32, name=f"weighted{t}") for t in range(PACK)]
        path = [keep.tile([P, U], F32, name=f"path{t}") for t in range(PACK)]
        suffixed = [keep.tile([P, U], F32, name=f"suffixed{t}") for t in range(PACK)]
        sibling = {t: keep.tile([P, U], F32, name=f"sibling{t}") for t in range(FUSED, PACK)}

        def gate(t):
            nc.vector.tensor_tensor(
                by_member(root_window[t][:, V:]),
                y[t][:].rearrange("p (v d) -> p d v", d=2),
                by_member(leaf_window[t][:, V:]),
                ALU.mult,
            )

        def pair_sum(t):
            nc.vector.tensor_tensor(root_window[t][:, :V], root_window[t][:, V : 2 * V], root_window[t][:, 2 * V :], ALU.add)

        def scale_nodes(t):
            nc.vector.tensor_scalar(leaf_window[t][:, :V], root_window[t][:, :V], unit_sb[:, t : t + 1], None, ALU.mult)

        def fetch(out, window, offsets):
            nc.scalar.activation(out, window[:].indirect(offsets), ACT.Copy)

        def look_up(t):
            fetch(rt[t][:], root_window[t], root_sb[:])
            if t > 0:
                fetch(lf[t][:], leaf_window[t] if t < FUSED else root_window[t], leaf_sb[:])
            nc.scalar.activation(th[t][:], rt[t][:], ACT.Tanh)

        def weigh(t, cols):
            nc.vector.tensor_tensor(weighted[t][:, cols], lf[t][:, cols], th[t][:, cols], ALU.mult)

        def join(t, cols):
            if t < FUSED:
                nc.vector.scalar_tensor_tensor(
                    path[t][:, cols], rt[t][:, cols], unit_sb[:, t : t + 1], weighted[t][:, cols], ALU.mult, ALU.add
                )
            else:
                nc.vector.tensor_tensor(path[t][:, cols], rt[t][:, cols], weighted[t][:, cols], ALU.add)

        def suffix(t, cols):
            if t < FUSED:
                nc.vector.tensor_tensor(suffixed[t][:, cols], path[t][:, cols], own_sb[:, t, cols], ALU.mult)
            else:
                nc.vector.scalar_tensor_tensor(
                    suffixed[t][:, cols], path[t][:, cols], unit_sb[:, t : t + 1], own_sb[:, t, cols], ALU.mult, ALU.mult
                )

        def add_sibling(t, k):
            cols = halves[k]
            if t < FUSED:
                nc.vector.tensor_tensor(hid[k][:, t, :], lf[t][:].indirect(sib_halves[k]), suffixed[t][:, cols], ALU.add)
            else:
                nc.vector.scalar_tensor_tensor(
                    hid[k][:, t, :], sibling[t][:, cols], unit_sb[:, t : t + 1], suffixed[t][:, cols], ALU.mult, ALU.add
                )

        out_codes = keep.tile([P, U], U32, name="out_codes", align_bytes=64)
        out_scales = keep.tile([P, U], U8, name="out_scales", align_bytes=64)
        hid_codes = keep.tile([P, U], U32, name="hid_codes", align_bytes=64)
        hid_scales = keep.tile([P, U], U8, name="hid_scales", align_bytes=64)
        out_rows = out_0.rearrange("(p t) j -> p t j", t=PACK)
        out_words = out_1[0].rearrange("p c r -> p (c r)").bitcast(I32)
        hid_bf, res, res_bf = {}, {}, {}

        def interleave(copy, dst, src):
            copy(dst.rearrange("p (c i t) -> p c t i", i=2, t=PACK), src.rearrange("p t (c i) -> p c t i", i=2))

        def round_hidden(h, copy):
            k, start = divmod(h * CH, HALF)
            hid_bf[h] = keep.tile([P, CH * PACK], BF16, name=f"hid_bf{h}", align_bytes=64)
            interleave(copy, hid_bf[h][:], hid[k][:, :, start : start + CH])

        def last_product(h):
            cols = slice(h * CH, (h + 1) * CH)
            nc.vector.quantize_mx(out=hid_codes[:, cols].bitcast(FP8X4), scales=hid_scales[:, cols], in_=hid_bf[h][:])
            acc = psum.tile([P, PACK, CH], F32, name=f"acc{h}", tag=f"bank{h}")
            for t in range(PACK):
                nc.tensor.matmul_mx(
                    out=acc[:, t, :],
                    lhsT=w3w[:, 0, t, :].bitcast(FP4X4),
                    lhsT_scale=w3s[:, 0, t, :],
                    rhs=hid_codes[:, cols].bitcast(FP8X4),
                    rhs_scale=hid_scales[:, cols],
                    start=True,
                    stop=True,
                )
            res[h] = keep.tile([P, PACK, CH], F32, name=f"res{h}")
            nc.scalar.copy(res[h][:], acc[:])
            nc.sync.dma_start(out_rows[:, :, cols], res[h][:])

        def round_result(h):
            res_bf[h] = keep.tile([P, CH * PACK], BF16, name=f"res_bf{h}", align_bytes=64)
            interleave(nc.vector.tensor_copy, res_bf[h][:], res[h][:])

        def planes(h):
            cols = slice(h * CH, (h + 1) * CH)
            nc.vector.quantize_mx(out=out_codes[:, cols].bitcast(FP8X4), scales=out_scales[:, cols], in_=res_bf[h][:])
            if h % 2:
                nc.sync.dma_start(out_words[:, halves[h // 2]], out_codes[:, halves[h // 2]].bitcast(I32))

        gate(0)
        gate(1)
        pair_sum(0)
        pair_sum(1)
        scale_nodes(0)
        scale_nodes(1)
        w3s = deal(w3s_raw, 1, U8, 1, "w3s", "w3s")
        nc.vector.tensor_copy(lf[0][:], leaf_window[0][:].indirect(leaf_sb[:]))
        gate(2)
        look_up(0)
        look_up(1)
        weigh(0, whole)
        gate(3)
        join(0, whole)
        pair_sum(2)
        pair_sum(3)
        suffix(0, whole)
        look_up(2)
        look_up(3)
        for k in range(2):
            for t in range(FUSED, PACK):
                fetch(sibling[t][:, halves[k]], lf[t], sib_halves[k])
        for t in (1, 2):
            weigh(t, whole)
            add_sibling(t - 1, 0)
            join(t, whole)
            add_sibling(t - 1, 1)
            suffix(t, whole)
        weigh(3, halves[0])
        weigh(3, halves[1])
        join(3, halves[0])
        add_sibling(2, 0)
        suffix(3, halves[0])
        join(3, halves[1])
        add_sibling(3, 0)
        round_hidden(0, nc.scalar.copy)
        round_hidden(1, nc.scalar.copy)
        suffix(3, halves[1])
        add_sibling(2, 1)
        add_sibling(3, 1)
        last_product(0)
        round_hidden(2, nc.vector.tensor_copy)
        round_hidden(3, nc.scalar.copy)
        last_product(1)
        round_result(0)
        last_product(2)
        last_product(3)
        planes(0)
        round_result(1)
        round_result(2)
        planes(1)
        round_result(3)
        planes(2)
        planes(3)

        for q in range(4):
            queue = nc.scalar if q % 2 else nc.sync
            queue.dma_start(
                out_2[0, 4 * q : 4 * q + 4, :].bitcast(I32), out_scales[32 * q : 32 * q + 4, :].bitcast(I32)
            )
